import numpy as np
import ml_dtypes


def mxq(x, axis, fmt="e4m3"):
    dtype, down = {"e4m3": (ml_dtypes.float8_e4m3fn, 7), "e5m2": (ml_dtypes.float8_e5m2, 14)}[fmt]
    v = np.moveaxis(np.asarray(x, np.float32).astype(ml_dtypes.bfloat16).astype(np.float64), axis, -1)
    blocks = v.reshape(v.shape[:-1] + (-1, 32))
    amax = np.abs(blocks).max(-1, keepdims=True)
    byte = np.maximum(np.where(amax > 0, np.frexp(amax)[1] - 1 + 127, 0) - down, 1)
    scale = np.exp2(byte - 127.0)
    codes = (blocks / scale).astype(np.float32).astype(dtype).astype(np.float64)
    return np.moveaxis((codes * scale).reshape(v.shape), -1, axis)


WIDE = False


def mx_kscale(k):
    if not WIDE:
        return np.ones(k)
    levels = np.array([10, -10, 5, -5, 0])
    if k % 512:
        return np.exp2(np.random.permutation(np.resize(levels, k // 32))).repeat(32)
    a = np.empty((k // 512, 16))
    for p in range(k // 512):
        a[p, :8] = np.random.permutation(np.resize(levels, 8))
        for g in range(8):
            far = levels[np.abs(levels - a[p, g]) >= 10]
            a[p, g + 8] = far[np.random.randint(len(far))]
    return np.exp2(a.ravel()).repeat(32)


BF16 = ml_dtypes.bfloat16


def bf(x):
    return np.asarray(x, np.float32).astype(BF16)


def f64(x):
    return np.asarray(x).astype(np.float64)

def planes(Y):
    n, m = Y.shape
    b = f64(bf(Y)).reshape(n // 32, 32, m)
    amax = np.abs(b).max(1)
    byte = np.clip(np.where(amax > 0, np.frexp(amax)[1] - 1 + 127 - 7, 1), 1, 254)
    codes = (b * np.exp2(127.0 - byte)[:, None, :]).reshape(n, m).astype(np.float32).astype(ml_dtypes.float8_e4m3fn).view(np.uint8)
    words = codes.reshape(n // 512, 128, 4, m).transpose(0, 1, 3, 2)
    return np.ascontiguousarray(words), np.ascontiguousarray(byte.astype(np.uint8).reshape(n // 512, 16, m))


B, N, D, P, C = 2, 1024, 512, 3, 512


def setup_inputs():
    s = mx_kscale(D)
    t = mx_kscale(N)
    spread = 0.75 + 0.5 * np.random.random_sample((B, 1, 1))
    return {
        "e1": bf(np.random.standard_normal((B, N, D)) * s),
        "e2": bf(np.random.standard_normal((B, N, D)) / s),
        "pend": bf(np.random.standard_normal((B, N, P)) * spread),
        "pstart": bf(np.random.standard_normal((B, N, P)) * spread),
        "g": bf((1.0 + 0.1 * np.random.standard_normal(N)) * t),
        "x": bf(np.random.standard_normal((B, N, C)) * (16.0 / np.sqrt(N)) / t[None, :, None]),
    }


def similarity_topology(e1, e2):
    e1q = mxq(e1, 2, "e4m3")
    e2q = mxq(e2, 2, "e4m3")
    logits = (e1q @ e2q.transpose(0, 2, 1)) / np.sqrt(D)
    return 1.0 / (1.0 + np.exp(-logits))


def geometric_topology(pend, pstart):
    r = np.sum(np.abs(pend[:, :, None, :] - pstart[:, None, :, :]), axis=-1)
    centre = np.mean(r, axis=(1, 2), keepdims=True)
    sigma = np.sqrt(np.mean(np.square(r - centre), axis=(1, 2), keepdims=True))
    return np.exp(-np.power(r, 1.2) / (2.0 * sigma))


def core(e1, e2, pend, pstart, g, x):
    s = similarity_topology(f64(e1), f64(e2))
    t = geometric_topology(f64(pend), f64(pstart))
    a = s + t
    k = (a - np.mean(a, axis=-1, keepdims=True)) * f64(g)[None, None, :]
    return mxq(k, 2, "e4m3") @ mxq(f64(x), 1, "e4m3")


def reference(e1, e2, pend, pstart, g, x):
    R_out = core(e1, e2, pend, pstart, g, x)
    words, scales = planes(np.moveaxis(R_out, 1, 0).reshape(1024, -1))
    return R_out, words, scales

import math
from contextlib import ExitStack

import concourse.mybir as mybir
from concourse.masks import make_identity

B, N, D, C = 2, 1024, 512, 512
FLOPS = 2 * B * N * N * (D + C)

F32 = mybir.dt.float32
BF16 = mybir.dt.bfloat16
U32 = mybir.dt.uint32
I32 = mybir.dt.int32
U8 = mybir.dt.uint8
FP8 = mybir.dt.float8_e4m3fn_x4
ALU = mybir.AluOpType
ACT = mybir.ActivationFunctionType
AX = mybir.AxisListType

P = 128
T = 4
PA, PB = 5, 3
TANH_N = [8, 8, 8, 8, 8, 8, 9, 10, 11, 12, 12]
MM0 = {}
MM_AT = {0: 0, 1: 1, 2: 2, 3: 3, 9: 4, 11: 5, 13: 6, 15: 7}
RG0 = 6
CENT0 = (0, 1, 2, 3, 4, 5, 6, 7)
CENT1 = (0, 1, 2, 3, 4, 6)
LAG0, LAG1 = 2, 2


def weave(main, *sides):
    done = [0] * len(sides)
    for n, step in enumerate(main):
        step()
        for k, side in enumerate(sides):
            upto = len(side) * (n + 1) // len(main)
            for fill in side[done[k] : upto]:
                fill()
            done[k] = upto


def tile_topologicfusedlanetopologyaggregation_x1_kernel(tc, e1, e2, pend, pstart, g, x, out_0, out_1, out_2):
    nc = tc.nc
    with ExitStack() as ctx:
        keep = ctx.enter_context(tc.tile_pool(name="keep", bufs=1))
        work = ctx.enter_context(tc.tile_pool(name="work", bufs=2))
        psum = ctx.enter_context(tc.psum_pool(name="psum", bufs=1))

        warm = keep.tile([P, 2], F32, name="warm")
        ident = keep.tile([P, P], F32, name="ident")
        ones = keep.tile([P, P], F32, name="ones")
        pst = keep.tile([P, 2 * B, 16], BF16, name="pst")
        pen = keep.tile([P, 2 * B, 16], BF16, name="pen")
        gt = keep.tile([P, 2, 16], BF16, name="gt")
        raw = {}

        def load_raw(key, src, b, h):
            tl = work.tile([P, T, 512], BF16, name="raw_%s_%d_%d" % (key, b, h), tag="raw", bufs=3)
            nc.sync.dma_start(out=tl[:], in_=src[b, 512 * h : 512 * h + 512, :].rearrange("(p t) k -> p t k", t=T))
            raw[key, b, h] = tl

        def copy(eng, out, in_):
            if eng == "S":
                nc.scalar.copy(out=out, in_=in_)
            else:
                nc.vector.tensor_copy(out=out, in_=in_)

        pf = keep.tile([P, 2 * B, 12], F32, name="pf")
        ph = keep.tile([P, 2 * B, 12], F32, name="ph")
        pnf = keep.tile([P, 2 * B, 12], F32, name="pnf")
        asum = keep.tile([P, 2 * B, T], F32, name="asum")
        na = keep.tile([P, 2 * B, T], F32, name="na")
        gh = keep.tile([P, 2, T], F32, name="gh")
        bcs = {}

        bbank = {}

        def bcast_tr(b, gi, c):
            bank = psum.tile([P, T, P], F32, name="bc_%d_%d_%d" % (b, gi, c), tag="pb", bufs=PB)
            for t in range(T):
                k = 3 * t + c
                nc.tensor.transpose(bank[:, t, :], pnf[:, 2 * b + gi, k : k + 1].to_broadcast([P, P]), ident[:])
            bbank[b, gi, c] = bank

        def bcast_cp(b, gi, c, eng):
            if b not in bcs:
                bcs[b] = work.tile([P, 3, N], BF16, name="bcs%d" % b, tag="bcs", bufs=1)
            bank = bbank[b, gi, c]
            copy(eng, bcs[b][:, c, 512 * gi : 512 * gi + 512], bank[:].rearrange("p t i -> p (t i)"))

        codes = {}
        grps = {}

        ebank = {}

        def prep_tr(key, b, h, pair):
            if pair == 0:
                grps[key, b, h] = work.tile([P, 512, T], BF16, name="grp_%s_%d_%d" % (key, b, h), tag="grp", bufs=3, align_bytes=64)
            src = raw[key, b, h]
            bank = psum.tile([P, 2, 2, P], F32, name="et_%s_%d_%d_%d" % (key, b, h, pair), tag="pb", bufs=PB)
            for s in range(2):
                words = src[:, 2 * pair + s, :].bitcast(F32)
                for u in range(2):
                    nc.tensor.transpose(bank[:, s, u, :], words[:, u:256:2], ident[:])
            ebank[key, b, h, pair] = bank

        def prep_cp(key, b, h, pair, eng):
            grp = grps[key, b, h]
            bank = ebank[key, b, h, pair]
            dst = grp[:, 256 * pair : 256 * pair + 256, :].rearrange("p n j -> p (n j)").bitcast(F32)
            copy(eng, dst.rearrange("p (s r u) -> p s r u", s=2, u=2), bank[:].rearrange("p s u r -> p s r u"))

        def prep_q(key, b, h):
            if (key, b) not in codes:
                codes[key, b] = (
                    work.tile([P, N], U32, name="c_%s_%d" % (key, b), tag="c_" + key, bufs=1, align_bytes=64),
                    work.tile([P, N], U8, name="s_%s_%d" % (key, b), tag="s_" + key, bufs=1, align_bytes=64),
                )
            cd, sc = codes[key, b]
            cols = slice(512 * h, 512 * h + 512)
            nc.vector.quantize_mx(out=cd[:, cols].bitcast(FP8), scales=sc[:, cols], in_=grps[key, b, h][:].rearrange("p n j -> p (n j)"))

        th = {}
        sth = [keep.tile([P, 8, 2], F32, name="sth%d" % b) for b in range(B)]
        lgs = {}

        def logit(b, it, h):
            c1, s1 = codes["e1", b]
            c2, s2 = codes["e2", b]
            rows = slice(it * P, it * P + P)
            cols = slice(512 * h, 512 * h + 512)
            lg = psum.tile([P, 512], F32, name="lg_%d_%d_%d" % (b, it, h), tag="pb", bufs=PB)
            nc.tensor.matmul_mx(out=lg[:], lhsT=c1[:, rows].bitcast(FP8), lhsT_scale=s1[:, rows], rhs=c2[:, cols].bitcast(FP8), rhs_scale=s2[:, cols], start=True, stop=True)
            lgs[b, it, h] = lg

        def tanh(b, it, h):
            gi, tp = divmod(it, T)
            if (b, gi) not in th:
                th[b, gi] = work.tile([P, T, N], F32, name="th_%d_%d" % (b, gi), tag="th", bufs=3)
            nc.scalar.activation(out=th[b, gi][:, tp, 512 * h : 512 * h + 512], in_=lgs[b, it, h][:], func=ACT.Tanh, scale=0.5 / math.sqrt(D), accum_out=sth[b][:, it, h : h + 1])

        mp = {}

        def mprime(b, gi, h, k):
            if (b, gi, h) not in mp:
                mp[b, gi, h] = work.tile([P, 12, 512], F32, name="m_%d_%d_%d" % (b, gi, h), tag="m", bufs=3)
            q = 2 * b + h
            nc.vector.tensor_scalar(out=mp[b, gi, h][:, k, :], in0=bcs[b][:, k % 3, 512 * gi : 512 * gi + 512], scalar1=pf[:, q, k : k + 1], scalar2=ph[:, q, k : k + 1], op0=ALU.max, op1=ALU.subtract)

        lw = {}
        st = [keep.tile([P, 8, 2, 6], F32, name="st%d" % b) for b in range(B)]
        rb = {}

        def rsum(b, gi, h, tp):
            m = mp[b, gi, h]
            bank = psum.tile([P, T, P], F32, name="r_%d_%d_%d" % (b, T * gi + tp, h), tag="pa", bufs=PA)
            for t in range(T):
                for c in range(3):
                    nc.tensor.matmul(bank[:, t, :], lhsT=m[:, 3 * t + c, tp * P : tp * P + P], rhs=ident[:], is_transpose=True, start=(c == 0), stop=(c == 2))
            rb[b, gi, h, tp] = bank[:].rearrange("p t j -> p (t j)")

        def bn(b, gi, h, tp):
            nc.vector.bn_stats(out=st[b][:, T * gi + tp, h, :], in_=rb[b, gi, h, tp])

        def ln(b, gi, h, tp):
            if (b, gi) not in lw:
                lw[b, gi] = work.tile([P, T, N], F32, name="lw_%d_%d" % (b, gi), tag="lw", bufs=2)
            nc.scalar.activation(out=lw[b, gi][:, tp, 512 * h : 512 * h + 512], in_=rb[b, gi, h, tp], func=ACT.Ln, scale=2.0, bias=na[:, 2 * b + gi, tp : tp + 1])

        nsc = {}
        v4s = {}

        mv = [keep.tile([P, 8, 2], F32, name="mv%d" % b) for b in range(B)]

        def aggr(b, it):
            nc.vector.bn_aggr(out=mv[b][:, it, :], in_=st[b][:, it].rearrange("p h s -> p (h s)"))

        def sigma_a(b):
            ms = keep.tile([P, 2, 8], F32, name="ms%d" % b)
            sq = keep.tile([P, 8], F32, name="sq%d" % b)
            s2 = keep.tile([P, 2], F32, name="s2%d" % b)
            tot = psum.tile([P, 2], F32, name="tot%d" % b, tag="pb", bufs=PB)
            me = keep.tile([P, 2], F32, name="me%d" % b)
            vn = keep.tile([P, 1], F32, name="vn%d" % b)
            lv = keep.tile([P, 1], F32, name="lv%d" % b)
            nc.vector.scalar_tensor_tensor(out=ms[:, 0, :], in0=mv[b][:, :, 0], scalar=2.0, in1=na[:, 2 * b : 2 * b + 2, :].rearrange("p q t -> p (q t)"), op0=ALU.mult, op1=ALU.add)
            nc.vector.tensor_tensor(out=sq[:], in0=ms[:, 0, :], in1=ms[:, 0, :], op=ALU.mult)
            nc.vector.scalar_tensor_tensor(out=ms[:, 1, :], in0=mv[b][:, :, 1], scalar=4.0, in1=sq[:], op0=ALU.mult, op1=ALU.add)
            nc.vector.tensor_reduce(out=s2[:], in_=ms[:], axis=AX.X, op=ALU.add)
            nc.tensor.matmul(tot[:], lhsT=ones[:], rhs=s2[:], start=True, stop=True)
            nc.vector.tensor_scalar(out=me[:], in0=tot[:], scalar1=1.0 / N, scalar2=None, op0=ALU.mult)
            nc.vector.scalar_tensor_tensor(out=vn[:], in0=me[:, 0:1], scalar=me[:, 0:1], in1=me[:, 1:2], op0=ALU.mult, op1=ALU.subtract)
            nc.scalar.activation(out=lv[:], in_=vn[:], func=ACT.Ln, scale=-4.0)
            v4s[b] = (vn, lv)

        def sigma_b(b):
            vn, lv = v4s[b]
            y0 = keep.tile([P, 1], F32, name="y0%d" % b)
            y2 = keep.tile([P, 1], F32, name="y2%d" % b)
            y3 = keep.tile([P, 1], F32, name="y3%d" % b)
            yh = keep.tile([P, 1], F32, name="yh%d" % b)
            ns = keep.tile([P, 1], F32, name="ns%d" % b)
            nsc[b] = ns
            nc.scalar.activation(out=y0[:], in_=lv[:], func=ACT.Exp, scale=-0.5)
            return [
                lambda: nc.vector.tensor_tensor(out=y2[:], in0=y0[:], in1=y0[:], op=ALU.mult),
                lambda: nc.vector.scalar_tensor_tensor(out=y3[:], in0=y2[:], scalar=vn[:], in1=y0[:], op0=ALU.mult, op1=ALU.mult),
                lambda: nc.vector.tensor_scalar(out=yh[:], in0=y3[:], scalar1=-2.0, scalar2=None, op0=ALU.mult),
                lambda: nc.vector.scalar_tensor_tensor(out=ns[:], in0=y0[:], scalar=-1.5, in1=yh[:], op0=ALU.mult, op1=ALU.add),
            ]

        def pow12(b, gi, k):
            blk = lw[b, gi][:, 2 * k : 2 * k + 2, :]
            nc.scalar.activation(out=blk, in_=blk, func=ACT.Exp, scale=1.2)

        xc = {}

        def x_copy(b, h):
            grps["x", b, h] = work.tile([P, C, T], BF16, name="grp_x_%d_%d" % (b, h), tag="grp", bufs=3, align_bytes=64)
            nc.vector.tensor_copy(out=grps["x", b, h][:].rearrange("p (c i) t -> p c t i", i=4), in_=raw["x", b, h][:].rearrange("p t (c i) -> p c t i", i=4))

        def x_q(b, h):
            cd = keep.tile([P, C], U32, name="xc_%d_%d" % (b, h), align_bytes=64)
            sc = keep.tile([P, C], U8, name="xs_%d_%d" % (b, h), align_bytes=64)
            nc.vector.quantize_mx(out=cd[:].bitcast(FP8), scales=sc[:], in_=grps["x", b, h][:].rearrange("p c t -> p (c t)"))
            xc[b, h] = (cd, sc)

        stt = [keep.tile([P, 8], F32, name="stt%d" % b) for b in range(B)]
        sths = [keep.tile([P, 8], F32, name="sths%d" % b) for b in range(B)]
        nm = [keep.tile([P, 8], F32, name="nm%d" % b) for b in range(B)]
        kg = {}
        ab = {}

        def thsum(b):
            nc.vector.tensor_tensor(out=sths[b][:], in0=sth[b][:, :, 0], in1=sth[b][:, :, 1], op=ALU.add)

        def texp(b, it):
            gi, tp = divmod(it, T)
            row = lw[b, gi][:, tp, :]
            nc.scalar.activation(out=row, in_=row, func=ACT.Exp, scale=nsc[b][:], bias=math.log(2.0), accum_out=stt[b][:, it : it + 1])

        def rowmean(b, it):
            one = slice(it, it + 1)
            nc.vector.tensor_scalar(out=nm[b][:, one], in0=stt[b][:, one], scalar1=sths[b][:, one], scalar2=-1.0 / N, op0=ALU.add, op1=ALU.mult)

        def center(b, it):
            gi, tp = divmod(it, T)
            row = lw[b, gi][:, tp, :]
            nc.vector.tensor_scalar(out=row, in0=row, scalar1=nm[b][:, it : it + 1], scalar2=None, op0=ALU.add)

        def asum_t(b, it, h, centered):
            gi, tp = divmod(it, T)
            bank = psum.tile([P, T, P], F32, name="a_%d_%d_%d" % (b, it, h), tag="pa", bufs=PA)
            for t in range(T):
                cols = slice(512 * h + t * P, 512 * h + t * P + P)
                parts = [th[b, gi][:, tp, cols], lw[b, gi][:, tp, cols]]
                if not centered:
                    parts.append(nm[b][:, it : it + 1].to_broadcast([P, P]))
                for k in range(len(parts)):
                    nc.tensor.matmul(bank[:, t, :], lhsT=parts[k], rhs=ident[:], is_transpose=True, start=(k == 0), stop=(k == len(parts) - 1))
            ab[b, it, h] = bank

        def gain(b, it, h):
            gi, tp = divmod(it, T)
            if (b, gi, h) not in kg:
                kg[b, gi, h] = work.tile([P, 512, T], BF16, name="kg_%d_%d_%d" % (b, gi, h), tag="kg", bufs=2, align_bytes=64)
            nc.vector.tensor_tensor(out=kg[b, gi, h][:, tp * P : tp * P + P, :], in0=ab[b, it, h][:].rearrange("p t i -> p i t"), in1=gh[:, h, :].unsqueeze(1).to_broadcast([P, P, T]), op=ALU.mult)

        kc = {}
        o32 = {}

        def quant_k(b, gi, h, lo, hi):
            if (b, gi, h) not in kc:
                kc[b, gi, h] = (
                    work.tile([P, 512], U32, name="kc_%d_%d_%d" % (b, gi, h), tag="kc%d" % h, bufs=2, align_bytes=64),
                    work.tile([P, 512], U8, name="ks_%d_%d_%d" % (b, gi, h), tag="ks%d" % h, bufs=2, align_bytes=64),
                )
            cd, sc = kc[b, gi, h]
            cols = slice(lo * P, hi * P)
            nc.vector.quantize_mx(out=cd[:, cols].bitcast(FP8), scales=sc[:, cols], in_=kg[b, gi, h][:, cols, :].rearrange("p i t -> p (i t)"))

        accs = {}

        def mm2(b, gi, tp):
            rows = slice(tp * P, tp * P + P)
            acc = psum.tile([P, C], F32, name="acc_%d_%d_%d" % (b, gi, tp), tag="pb", bufs=PB)
            for h in range(2):
                kcd, ksc = kc[b, gi, h]
                xcd, xsc = xc[b, h]
                nc.tensor.matmul_mx(out=acc[:], lhsT=kcd[:, rows].bitcast(FP8), lhsT_scale=ksc[:, rows], rhs=xcd[:].bitcast(FP8), rhs_scale=xsc[:], start=(h == 0), stop=(h == 1))
            accs[b, gi, tp] = acc

        def out_copy(b, gi, tp, eng):
            if (b, gi) not in o32:
                o32[b, gi] = work.tile([P, T, C], F32, name="o32_%d_%d" % (b, gi), tag="m" if b else "o32", bufs=3 if b else 1)
            copy(eng, o32[b, gi][:, tp, :], accs[b, gi, tp][:])

        def out_regroup(b, gi):
            res = o32[b, gi]
            nc.sync.dma_start(out=out_0[b, 512 * gi : 512 * gi + 512, :].rearrange("(p t) c -> p t c", t=T), in_=res[:])
            grps["o", b, gi] = work.tile([P, C, T], BF16, name="grp_o_%d_%d" % (b, gi), tag="grp", bufs=3, align_bytes=64)
            nc.vector.tensor_copy(out=grps["o", b, gi][:], in_=res[:].rearrange("p t c -> p c t"))

        def out_quant(b, gi):
            cd = work.tile([P, C], U32, name="oc_%d_%d" % (b, gi), tag="oc", bufs=2, align_bytes=64)
            sc = work.tile([P, C], U8, name="os_%d_%d" % (b, gi), tag="os", bufs=2, align_bytes=64)
            nc.vector.quantize_mx(out=cd[:].bitcast(FP8), scales=sc[:], in_=grps["o", b, gi][:].rearrange("p c t -> p (c t)"))
            nc.sync.dma_start(out=out_1[gi, :, C * b : C * b + C, :].rearrange("p m f -> p (m f)").bitcast(I32), in_=cd[:].bitcast(I32))
            for q in range(4):
                nc.sync.dma_start(out=out_2[gi, 4 * q : 4 * q + 4, C * b : C * b + C].bitcast(I32), in_=sc[32 * q : 32 * q + 4, :].bitcast(I32))

        with tc.manual_schedule():
            nc.sync.dma_start(out=pen[:, :, 0:12], in_=pend.rearrange("b n c -> (b n) c").rearrange("(q p t) c -> p q (t c)", p=P, t=T))
            nc.sync.dma_start(out=pst[:, :, 0:12], in_=pstart.rearrange("b n c -> (b n) c").rearrange("(q p t) c -> p q (t c)", p=P, t=T))
            load_raw("e2", e2, 0, 0)
            load_raw("e1", e1, 0, 0)
            load_raw("e2", e2, 0, 1)
            nc.sync.dma_start(out=gt[:, :, 0:4], in_=g.rearrange("(h p t) -> p h t", p=P, t=T))
            load_raw("e1", e1, 0, 1)
            nc.vector.memset(warm[:], 0.0)
            make_identity(nc, ident[:])
            nc.gpsimd.memset(ones[:], 1.0)
            nc.scalar.activation(out=warm[:, 1:2], in_=warm[:, 0:1], func=ACT.Exp)
            nc.vector.tensor_copy(out=pnf[:], in_=pen[:, :, 0:12])
            nc.vector.tensor_copy(out=pf[:], in_=pst[:, :, 0:12])
            nc.vector.tensor_scalar(out=ph[:], in0=pst[:, :, 0:12], scalar1=0.5, scalar2=None, op0=ALU.mult)
            pen4 = pen[:, :, 0:12].rearrange("p q (t c) -> p q t c", c=3)
            nc.vector.tensor_tensor(out=asum[:], in0=pen4[:, :, :, 0], in1=pen4[:, :, :, 1], op=ALU.add)

            def M(b, n):
                gi, h = divmod(n, 2)
                return [lambda k=k: mprime(b, gi, h, k) for k in range(12)]

            def R(b):
                return [(b, gi, h, tp) for gi in range(2) for h in range(2) for tp in range(T)]

            halves = [("e2", 0), ("e1", 0), ("e2", 1), ("e1", 1)]
            ebanks = [(key, h, pair) for key, h in halves for pair in range(2)]
            bcl = [(gi, c) for gi in range(2) for c in range(3)]
            LG = [(it, h) for it in range(8) for h in range(2)]

            def etr(b, n):
                key, h, pair = ebanks[n]
                prep_tr(key, b, h, pair)

            def ecp(b, n, eng):
                key, h, pair = ebanks[n]
                prep_cp(key, b, h, pair, eng)

            def eq(b, n):
                prep_q(halves[n][0], b, halves[n][1])

            for n in range(6):
                bcast_tr(0, *bcl[n])
                bcast_cp(0, *bcl[n], "SV"[n % 2])
            nc.vector.scalar_tensor_tensor(out=na[:], in0=asum[:], scalar=-1.0, in1=pen4[:, :, :, 2], op0=ALU.mult, op1=ALU.subtract)
            m0 = M(0, 0) + M(0, 1)
            for n in range(8):
                etr(0, n)
                ecp(0, n, "S")
                for f in m0[2 * n : 2 * n + 2]:
                    f()
                if n % 2:
                    eq(0, n // 2)
            load_raw("x", x, 0, 0)
            load_raw("x", x, 0, 1)
            for key, h in halves:
                load_raw(key, e1 if key == "e1" else e2, 1, h)
            for h in range(2):
                load_raw("x", x, 1, h)
            nc.vector.tensor_scalar(out=gh[:], in0=gt[:, :, 0:4], scalar1=0.5, scalar2=None, op0=ALU.mult)

            def bn_aggr(b, gi, h, tp):
                bn(b, gi, h, tp)
                if h == 1:
                    aggr(b, T * gi + tp)

            r0 = R(0)
            v2 = m0[16:] + [lambda: x_copy(0, 0)] + M(0, 2)[:6] + [lambda: x_copy(0, 1)] + [lambda: x_q(0, 0)] + M(0, 2)[6:] + [lambda: x_q(0, 1)]
            logit(0, *LG[0])
            logit(0, *LG[1])
            for n in range(16):
                tanh(0, *LG[n])
                if n + 2 < 16:
                    logit(0, *LG[n + 2])
                if n % 2 and n // 2 < PA:
                    rsum(*r0[n // 2])
                for f in v2[2 * n : 2 * n + 2]:
                    f()
                if n % 2 == 0 and 1 <= n // 2 <= PA:
                    bn_aggr(*r0[n // 2 - 1])

            def ln_phase(b, before, after):
                r = R(b)
                m3 = M(b, 3)
                for n in range(16):
                    before(n)
                    if n < 6:
                        m3[2 * n]()
                        m3[2 * n + 1]()
                    if n + PA < 16:
                        rsum(*r[n + PA])
                    ln(*r[n])
                    after(n)
                    if n + PA < 16:
                        bn_aggr(*r[n + PA])

            aggr_late = {}
            et_at = {1: 0, 3: 1, 5: 2, 7: 3, 10: 4, 12: 5, 14: 6, 15: 7}

            def b0(n):
                if n in et_at:
                    etr(1, et_at[n])

            def a0(n):
                k = et_at.get(n - 2)
                if k is not None:
                    ecp(1, k, "S")
                    if k % 2:
                        eq(1, k // 2)

            ln_phase(0, b0, a0)
            ecp(1, 6, "S")
            ecp(1, 7, "S")
            sigma_a(0)
            chain = sigma_b(0)
            m1 = M(1, 0) + M(1, 1)
            eq(1, 3)
            for n in range(6):
                bcast_tr(1, *bcl[n])
            v4 = []
            for n in range(6):
                v4.append(lambda n=n: bcast_cp(1, *bcl[n], "V"))
            for k in range(4):
                v4.insert(2 * k + 1, chain[k])
            logit(1, *LG[0])
            logit(1, *LG[1])

            def pt(n):
                def run():
                    if n % 3 == 0:
                        pow12(0, n // 3 // 2, n // 3 % 2)
                    else:
                        k = n - n // 3 - 1
                        tanh(1, *LG[k])
                        logit(1, *LG[k + 2])
                return run

            weave([pt(n) for n in range(12)], v4 + m1 + M(1, 2))
            thsum(0)

            def t_phase(b, tiles, lead, extra, centered, lag, after_gain):
                n_t = len(tiles)
                for n in range(n_t + lag):
                    lead(n)
                    if n < n_t:
                        texp(b, tiles[n])
                    prev = tiles[n - 1] if 1 <= n <= n_t else None
                    old = tiles[n - lag] if n >= lag else None
                    if prev is not None:
                        rowmean(b, prev)
                    if old is not None:
                        gain(b, old, 0)
                    if prev is not None and prev in centered:
                        center(b, prev)
                    if old is not None:
                        gain(b, old, 1)
                        after_gain(b, old)
                    if prev is not None:
                        for h in range(2):
                            asum_t(b, prev, h, prev in centered)
                    extra(n)

            def quant_4(b, it):
                gi, tp = divmod(it, T)
                if tp == T - 1:
                    for h in range(2):
                        quant_k(b, gi, h, 0, T)

            def quant_fine(b, it):
                gi, tp = divmod(it, T)
                if tp:
                    for h in range(2):
                        quant_k(b, gi, h, 0 if tp == 1 else tp, tp + 1)

            tanh_n = TANH_N

            def lead0(n):
                for k in range(tanh_n[n] + 2, tanh_n[n + 1] + 2):
                    if k < 16:
                        logit(1, *LG[k])

            def extra0(n):
                for k in range(tanh_n[n], tanh_n[n + 1]):
                    tanh(1, *LG[k])
                if n in MM0:
                    mm2(0, 0, MM0[n])
                if n - 1 in MM0:
                    out_copy(0, 0, MM0[n - 1], "S")

            t_phase(0, list(range(8)), lead0, extra0, CENT0, LAG0, quant_4)
            r1 = R(1)
            for n in range(PA):
                if TANH_N[-1] + n < 16:
                    tanh(1, *LG[TANH_N[-1] + n])
                if TANH_N[-1] + n + 2 < 16:
                    logit(1, *LG[TANH_N[-1] + n + 2])
                rsum(*r1[n])
                bn_aggr(*r1[n])
            mm_at = MM_AT

            def b1(n):
                if n in mm_at:
                    mm2(0, *divmod(mm_at[n], T))

            def a1(n):
                k = mm_at.get(n - 2)
                if k is not None:
                    out_copy(0, *divmod(k, T), "S")
                if n == RG0:
                    out_regroup(0, 0)
                if n == RG0 + 1:
                    out_quant(0, 0)

            ln_phase(1, b1, a1)
            out_copy(0, 1, 3, "S")
            sigma_a(1)
            chain = sigma_b(1)
            out_regroup(0, 1)
            for f in chain:
                f()
            out_quant(0, 1)
            pow12(1, 0, 0)
            pow12(1, 0, 1)
            x_copy(1, 0)
            x_copy(1, 1)
            x_q(1, 0)
            x_q(1, 1)
            thsum(1)

            def lead_g0(n):
                if n == 4:
                    pow12(1, 1, 0)
                    pow12(1, 1, 1)

            def none(n):
                return None

            def extra_g1(n):
                if n < 4:
                    out_copy(1, 0, n, "S")

            t_phase(1, [0, 1, 2, 3], lead_g0, none, CENT1, LAG1, quant_4)
            mm2(1, 0, 0)
            mm2(1, 0, 1)
            t_phase(1, [4, 5, 6, 7], lambda n: mm2(1, 0, n + 1) if n in (1, 2) else None, extra_g1, CENT1, LAG1, quant_fine)
            for tp in range(T):
                mm2(1, 1, tp)
                out_copy(1, 1, tp, "S")
            out_regroup(1, 0)
            out_quant(1, 0)
            out_regroup(1, 1)
            out_quant(1, 1)
